import numpy as np
import ml_dtypes


def mxq(x, axis, fmt="e4m3"):
    dtype, down = {"e4m3": (ml_dtypes.float8_e4m3fn, 7), "e5m2": (ml_dtypes.float8_e5m2, 14)}[fmt]
    v = np.moveaxis(np.asarray(x, np.float32).astype(ml_dtypes.bfloat16).astype(np.float64), axis, -1)
    blocks = v.reshape(v.shape[:-1] + (-1, 32))
    amax = np.abs(blocks).max(-1, keepdims=True)
    byte = np.maximum(np.where(amax > 0, np.frexp(amax)[1] - 1 + 127, 0) - down, 1)
    scale = np.exp2(byte - 127.0)
    codes = (blocks / scale).astype(np.float32).astype(dtype).astype(np.float64)
    return np.moveaxis((codes * scale).reshape(v.shape), -1, axis)


WIDE = False


def mx_kscale(k):
    if not WIDE:
        return np.ones(k)
    levels = np.array([10, -10, 5, -5, 0])
    if k % 512:
        return np.exp2(np.random.permutation(np.resize(levels, k // 32))).repeat(32)
    a = np.empty((k // 512, 16))
    for p in range(k // 512):
        a[p, :8] = np.random.permutation(np.resize(levels, 8))
        for g in range(8):
            far = levels[np.abs(levels - a[p, g]) >= 10]
            a[p, g + 8] = far[np.random.randint(len(far))]
    return np.exp2(a.ravel()).repeat(32)


def f64(x):
    return np.asarray(x).astype(np.float64)


def striped(idx):
    return np.tile(idx.reshape(-1, 16).T, (8, 1)).astype(np.uint16)


def unstriped(offs):
    return offs[:16].T.reshape(-1).astype(np.int64)


def striped8(idx):
    return np.concatenate([x.reshape(-1, 16).T for x in idx]).astype(np.uint16)


def runs(offs, k):
    lists = np.stack([offs[16 * r : 16 * r + 16].T.reshape(-1) for r in range(8)]).astype(np.int64)
    return lists[np.arange(k) % 512 // 64]


def pack_weight(w):
    k, n = w.shape
    w = f64(np.asarray(w, np.float32).astype(ml_dtypes.bfloat16)).reshape(k // 32, 32, n)
    amax = np.abs(w).max(1)
    byte = np.clip(np.where(amax > 0, np.frexp(amax)[1] - 1 + 127 - 7, 1), 1, 254)
    scaled = (w * np.exp2(127.0 - byte)[:, None, :]).reshape(k, n).astype(np.float32)
    words = np.ascontiguousarray(scaled.reshape(k // 512, 128, 4, n).transpose(0, 1, 3, 2)).astype(ml_dtypes.float8_e4m3fn).view(np.uint8)
    return words, np.ascontiguousarray(byte.astype(np.uint8).reshape(k // 512, 16, n))


def unpack_weight(words, scales):
    g, p, n, _ = words.shape
    vals = np.ascontiguousarray(words).view(ml_dtypes.float8_e4m3fn).astype(np.float64) * np.repeat(np.exp2(scales.astype(np.float64) - 127.0), 8, axis=1)[..., None]
    return vals.transpose(0, 1, 3, 2).reshape(g * 512, n)

def planes(y):
    n, m = y.shape
    v = y.astype(np.float32).astype(ml_dtypes.bfloat16).astype(np.float64).reshape(n // 32, 32, m)
    top = np.abs(v).max(1)
    byte = np.clip(np.where(top > 0, np.frexp(top)[1] - 1 + 127 - 7, 1), 1, 254)
    codes = (v * np.exp2(127.0 - byte)[:, None, :]).reshape(n, m).astype(np.float32).astype(ml_dtypes.float8_e4m3fn).view(np.uint8)
    words = codes.reshape(n // 512, 128, 4, m).transpose(0, 1, 3, 2)
    return np.ascontiguousarray(words), np.ascontiguousarray(byte.astype(np.uint8).reshape(n // 512, 16, m))


K, T, S, G, H, W, C = 512, 1024, 256, 2048, 512, 128, 512


def setup_inputs():
    n = np.random.standard_normal
    s = mx_kscale(K)[:, None]
    packed_xT = pack_weight(n((K, T)) * s)
    packed_dT = pack_weight(n((K, G)) / s)
    perm = np.random.permutation(S)
    return {
        "x_words": packed_xT[0],
        "x_scales": packed_xT[1],
        "d_words": packed_dT[0],
        "d_scales": packed_dT[1],
        "gs": (np.random.uniform(0.5, 1.5, (K, 1)) / s).astype(np.float32),
        "offs": striped8(np.random.randint(0, T, (8, S))),
        "k1": striped8(np.random.randint(0, G, (8, H))),
        "n1": striped(perm[:W]),
        "n2": striped(perm[W:]),
        "n3": striped(np.random.permutation(S)),
        "cand": striped8(np.random.randint(0, T, (8, C))),
        "n4": striped(np.random.permutation(S)),
        "n5": striped(np.random.permutation(S)),
    }


def reference(x_words, x_scales, d_words, d_scales, gs, offs, k1, n1, n2, n3, cand, n4, n5):
    x_cand = unpack_weight(x_words, x_scales)[np.arange(K)[:, None], runs(cand, K)]
    d_k1 = unpack_weight(d_words, d_scales)[np.arange(K)[:, None], runs(k1, K)]
    xq = unpack_weight(x_words, x_scales)[np.arange(K)[:, None], runs(offs, K)]
    h = 0.0625 * (d_k1.T @ xq)
    pa = h[:, unstriped(n1)]
    pb = h[:, unstriped(n2)]
    rb = pa - pb
    ds = np.zeros((H, S))
    ds[:, unstriped(n1)] = pb
    dt = ds.copy()
    dt[:, unstriped(n2)] = rb
    z = f64(gs) * (np.maximum(dt, 0.5 * dt[:, unstriped(n3)]))
    s = 0.0625 * ((x_cand.T @ mxq(z, 0, "e4m3")))
    st = np.maximum(s, s[:, unstriped(n4)])
    ds2 = np.zeros((C, S))
    ds2[:, unstriped(n5)] = st
    out_0 = ds2 - s
    return (out_0,) + planes(out_0)

@@ -1,0 +1,258 @@
+from contextlib import ExitStack
+
+import concourse.mybir as mybir
+
+K, T, S, G, H, W, C = 512, 1024, 256, 2048, 512, 128, 512
+FLOPS = 2 * K * H * S + 2 * K * C * S
+
+F32 = mybir.dt.float32
+BF16 = mybir.dt.bfloat16
+I32 = mybir.dt.int32
+U32 = mybir.dt.uint32
+U16 = mybir.dt.uint16
+U8 = mybir.dt.uint8
+FP8X4 = mybir.dt.float8_e4m3fn_x4
+ALU = mybir.AluOpType
+COPY = mybir.ActivationFunctionType.Copy
+
+P = 128
+PACK = 4
+HALF = S // 2
+
+
+def tile_picked_hpqhswapdsendhop_none_po_kernel(
+    tc, x_words, x_scales, d_words, d_scales, gs, offs, k1, n1, n2, n3, cand, n4, n5, out_0, out_1, out_2
+):
+    nc = tc.nc
+    with ExitStack() as ctx:
+        lists = ctx.enter_context(tc.tile_pool(name="lists", bufs=1))
+        sb = ctx.enter_context(tc.tile_pool(name="sb", bufs=1))
+        ps = ctx.enter_context(tc.psum_pool(name="ps", bufs=1))
+
+        def load_list(src, name):
+            t = lists.tile(list(src.shape), U16, name=name)
+            nc.sync.dma_start(t[:], src)
+            return t
+
+        def entries(lst, first, count):
+            return lst[:, first // 16 : (first + count) // 16]
+
+        d_sc_win = sb.tile([P, G], U8, name="d_sc_win", align_bytes=64)
+        x_sc_win = sb.tile([P, T], U8, name="x_sc_win", align_bytes=64)
+        nc.vector.memset(d_sc_win[:].bitcast(I32), 0)
+        nc.gpsimd.memset(x_sc_win[:].bitcast(I32), 0)
+        nc.scalar.dma_start(d_sc_win[0:P:8, :].bitcast(I32), d_scales[0].bitcast(I32))
+        nc.scalar.dma_start(x_sc_win[0:P:8, :].bitcast(I32), x_scales[0].bitcast(I32))
+
+        l_k1 = load_list(k1, "l_k1")
+        l_offs = load_list(offs, "l_offs")
+        gs_raw = sb.tile([P, PACK], F32, name="gs_raw")
+        nc.sync.dma_start(gs_raw[:], gs.rearrange("(p t) o -> p (t o)", t=PACK))
+        d_win = sb.tile([P, G], I32, name="d_win", align_bytes=64)
+        x_win = sb.tile([P, T], I32, name="x_win", align_bytes=64)
+        nc.sync.dma_start(d_win[:], d_words[0].rearrange("p n t -> p (n t)").bitcast(I32))
+        nc.sync.dma_start(x_win[:], x_words[0].rearrange("p n t -> p (n t)").bitcast(I32))
+        l_n2 = load_list(n2, "l_n2")
+        l_n1 = load_list(n1, "l_n1")
+        l_n3 = load_list(n3, "l_n3")
+        l_n4 = load_list(n4, "l_n4")
+        l_n5 = load_list(n5, "l_n5")
+        l_cand = load_list(cand, "l_cand")
+
+        gs16 = sb.tile([P, PACK], F32, name="gs16")
+        nc.scalar.activation(gs16[:], gs_raw[:], COPY, scale=0.0625)
+
+        first_rows = sb.tile([P, H + S], U8, name="first_rows", align_bytes=64)
+        cand_rows = sb.tile([P, C], U8, name="cand_rows", align_bytes=64)
+        nc.gpsimd.memset(first_rows[:].bitcast(I32), 0)
+        nc.gpsimd.memset(cand_rows[:].bitcast(I32), 0)
+
+        def move_rows(queue, dst, src):
+            for r in range(4):
+                queue.dma_start(dst[r:P:32, :].bitcast(I32), src[8 * r : P : 32, :].bitcast(I32))
+
+        def deal(dst, src, per_line, first, stop):
+            nc.vector.tensor_copy(
+                dst.rearrange("p (t a i) -> p a t i", t=PACK, i=per_line)[:, :, first:stop, :],
+                src.rearrange("p (a i t) -> p a t i", t=PACK, i=per_line)[:, :, first:stop, :],
+            )
+
+        first_bytes = sb.tile([P, H + S], U8, name="first_bytes", align_bytes=64)
+        nc.vector.tensor_copy(first_bytes[:, 0:H], d_sc_win[:].indirect(l_k1[:]))
+        nc.vector.tensor_copy(first_bytes[:, H : H + S], x_sc_win[:].indirect(l_offs[:]))
+        move_rows(nc.scalar, first_rows, first_bytes)
+
+        d_picked = sb.tile([P, H], U32, name="d_picked", align_bytes=64)
+        d_codes = sb.tile([P, H], U32, name="d_codes", align_bytes=64)
+        d_plane = sb.tile([P, H], U8, name="d_plane", align_bytes=64)
+        xq_codes = sb.tile([P, S], U32, name="xq_codes", align_bytes=64)
+        nc.vector.tensor_copy(d_picked[:], d_win[:].bitcast(U32).indirect(l_k1[:]))
+        nc.vector.tensor_copy(xq_codes[:], x_win[:].bitcast(U32).indirect(l_offs[:]))
+        deal(d_codes[:], d_picked[:], 4, 0, 1)
+        deal(d_plane[:], first_rows[:, 0:H], 16, 0, 1)
+        deal(d_codes[:], d_picked[:], 4, 1, PACK)
+        deal(d_plane[:], first_rows[:, 0:H], 16, 1, PACK)
+
+        h = []
+        for t in range(PACK):
+            acc = ps.tile([P, S], F32, name=f"h_acc{t}", tag=f"bank{t}")
+            nc.tensor.matmul_mx(
+                out=acc[:],
+                lhsT=d_codes[:, t * P : (t + 1) * P].bitcast(FP8X4),
+                lhsT_scale=d_plane[:, t * P : (t + 1) * P],
+                rhs=xq_codes[:].bitcast(FP8X4),
+                rhs_scale=first_rows[:, H : H + S],
+                start=True,
+                stop=True,
+            )
+            ht = sb.tile([P, S], F32, name=f"h{t}", align_bytes=64)
+            if t == 0:
+                nc.scalar.copy(ht[:], acc[:])
+            else:
+                nc.vector.tensor_copy(ht[:], acc[:])
+            h.append(ht)
+
+        c_codes = sb.tile([P, C], U32, name="c_codes", align_bytes=64)
+        c_dealt = sb.tile([P, C], U8, name="c_dealt", align_bytes=64)
+
+        def cand_bytes():
+            c_bytes = sb.tile([P, C], U8, name="c_bytes", tag="pa0", align_bytes=64)
+            for a in range(0, C, P):
+                nc.vector.tensor_copy(c_bytes[:, a : a + P], x_sc_win[:].indirect(entries(l_cand, a, P)))
+            deal(c_dealt[:], c_bytes[:], 16, 0, PACK)
+            move_rows(nc.sync, cand_rows, c_dealt)
+
+        def cand_words():
+            c_picked = sb.tile([P, C], U32, name="c_picked", tag="pa1", align_bytes=64)
+            for a in range(0, C, P):
+                nc.vector.tensor_copy(c_picked[:, a : a + P], x_win[:].bitcast(U32).indirect(entries(l_cand, a, P)))
+            deal(c_codes[:], c_picked[:], 4, 0, PACK)
+
+        pa = [sb.tile([P, W], F32, name=f"pa{t}", tag=f"pa{t}", align_bytes=64) for t in range(PACK)]
+        pb = [sb.tile([P, W], F32, name=f"pb{t}") for t in range(PACK)]
+        rb = [sb.tile([P, W], F32, name=f"rb{t}") for t in range(PACK)]
+        dt = []
+        hop = [sb.tile([P, S], F32, name=f"hop{t}") for t in range(PACK)]
+        top = [sb.tile([P, S], F32, name=f"top{t}") for t in range(PACK)]
+        z_bf = sb.tile([P, S, PACK], BF16, name="z_bf", align_bytes=64)
+        z_codes = sb.tile([P, S], U32, name="z_codes", align_bytes=64)
+        z_plane = sb.tile([P, S], U8, name="z_plane", align_bytes=64)
+        nc.gpsimd.memset(z_plane[:].bitcast(I32), 0)
+
+        def fetch_pairs(t):
+            nc.scalar.activation(pb[t][:], h[t][:].indirect(l_n2[:]), COPY)
+            nc.scalar.activation(pa[t][:], h[t][:].indirect(l_n1[:]), COPY)
+            nc.vector.tensor_tensor(rb[t][:], pa[t][:], pb[t][:], ALU.subtract)
+
+        def put_pb(t):
+            dt.append(sb.tile([P, S + 16], F32, name=f"dt{t}", tag="dt", bufs=2))
+            nc.scalar.activation(dt[t][:].indirect(l_n1[:]), pb[t][:], COPY)
+
+        def put_rb(t):
+            nc.scalar.activation(dt[t][:].indirect(l_n2[:]), rb[t][:], COPY)
+
+        def hop_half(t, u):
+            cols = slice(u * HALF, (u + 1) * HALF)
+            nc.scalar.activation(hop[t][:, cols], dt[t][:].indirect(entries(l_n3, u * HALF, HALF)), COPY)
+
+        def top_part(t, first, count):
+            cols = slice(first, first + count)
+            nc.vector.scalar_tensor_tensor(top[t][:, cols], hop[t][:, cols], 0.5, dt[t][:, cols], ALU.mult, ALU.max)
+
+        def z_part(t, first, count):
+            cols = slice(first, first + count)
+            nc.vector.tensor_scalar(z_bf[:, cols, t], top[t][:, cols], gs16[:, t : t + 1], None, ALU.mult)
+
+        def quantise_z(u):
+            cols = slice(u * HALF, (u + 1) * HALF)
+            nc.vector.quantize_mx(
+                out=z_codes[:, cols].bitcast(FP8X4),
+                scales=z_plane[:, cols],
+                in_=z_bf[:, cols, :].rearrange("p j t -> p (j t)"),
+            )
+
+        fetch_pairs(0)
+        put_pb(0)
+        for t in range(PACK):
+            if t + 1 < PACK:
+                fetch_pairs(t + 1)
+            put_rb(t)
+            if t + 1 < PACK:
+                put_pb(t + 1)
+                nc.scalar.activation(hop[t][:], dt[t][:].indirect(l_n3[:]), COPY)
+                top_part(t, 0, S)
+                z_part(t, 0, S)
+            if t == 0:
+                cand_bytes()
+            if t == 1:
+                cand_words()
+
+        s = [sb.tile([P, S + 16], F32, name=f"s{t}", align_bytes=64) for t in range(PACK)]
+
+        def score(t, first, count, bank):
+            cols = slice(first, first + count)
+            acc = ps.tile([P, count], F32, name=f"s_acc{t}_{first}", tag=f"bank{bank}")
+            nc.tensor.matmul_mx(
+                out=acc[:],
+                lhsT=c_codes[:, t * P : (t + 1) * P].bitcast(FP8X4),
+                lhsT_scale=cand_rows[:, t * P : (t + 1) * P],
+                rhs=z_codes[:, cols].bitcast(FP8X4),
+                rhs_scale=z_plane[:, cols],
+                start=True,
+                stop=True,
+            )
+            return acc
+
+        last = PACK - 1
+        for u in range(2):
+            hop_half(last, u)
+            top_part(last, u * HALF, HALF)
+        for u in range(2):
+            z_part(last, u * HALF, HALF)
+        for u in range(2):
+            quantise_z(u)
+            acc = score(0, u * HALF, HALF, 4 + u)
+            nc.scalar.activation(s[0][:, u * HALF : (u + 1) * HALF], acc[:], COPY, scale=0.0625)
+        for t in range(1, PACK):
+            acc = score(t, 0, S, (5 + t) % 8)
+            nc.vector.tensor_scalar(s[t][:, 0:S], acc[:], 0.0625, None, ALU.mult)
+
+        far = [sb.tile([P, S], F32, name=f"far{t}") for t in range(PACK)]
+        st = [sb.tile([P, S], F32, name=f"st{t}") for t in range(PACK)]
+        sent = [sb.tile([P, S + 96], F32, name=f"sent{t}") for t in range(PACK)]
+        y = [sb.tile([P, S], F32, name=f"y{t}") for t in range(PACK)]
+        y_bf = sb.tile([P, S, PACK], BF16, name="y_bf", align_bytes=64)
+        y_codes = sb.tile([P, S], U32, name="y_codes", align_bytes=64)
+        y_plane = sb.tile([P, S], U8, name="y_plane", align_bytes=64)
+        out_rows = out_0.rearrange("(p t) j -> p t j", t=PACK)
+
+        def fetch_far(t):
+            nc.scalar.activation(far[t][:], s[t][:].indirect(l_n4[:]), COPY)
+            nc.vector.tensor_tensor(st[t][:], far[t][:], s[t][:, 0:S], ALU.max)
+
+        def send(t):
+            nc.scalar.activation(sent[t][:].indirect(l_n5[:]), st[t][:], COPY)
+            parts = [slice(0, S)] if t < last else [slice(0, HALF), slice(HALF, S)]
+            for cols in parts:
+                nc.vector.tensor_tensor(y[t][:, cols], sent[t][:, cols], s[t][:, cols], ALU.subtract)
+            nc.sync.dma_start(out_rows[:, t, :], y[t][:])
+            for cols in parts:
+                nc.vector.tensor_copy(y_bf[:, cols, t], y[t][:, cols])
+
+        fetch_far(0)
+        for t in range(PACK):
+            if t + 1 < PACK:
+                fetch_far(t + 1)
+            send(t)
+
+        for u in range(2):
+            cols = slice(u * HALF, (u + 1) * HALF)
+            nc.vector.quantize_mx(
+                out=y_codes[:, cols].bitcast(FP8X4),
+                scales=y_plane[:, cols],
+                in_=y_bf[:, cols, :].rearrange("p j t -> p (j t)"),
+            )
+        nc.sync.dma_start(out_1[0].rearrange("p n t -> p (n t)").bitcast(I32), y_codes[:].bitcast(I32))
+        for q in range(4):
+            queue = nc.scalar if q < 3 else nc.sync
+            queue.dma_start(out_2[0, 4 * q : 4 * q + 4, :].bitcast(I32), y_plane[32 * q : 32 * q + 4, :].bitcast(I32))

@@ -18,6 +18,7 @@ COPY = mybir.ActivationFunctionType.Copy
 P = 128
 PACK = 4
 HALF = S // 2
+EARLY = G // 4
 
 
 def tile_picked_hpqhswapdsendhop_none_po_kernel(
@@ -41,35 +42,34 @@ def tile_picked_hpqhswapdsendhop_none_po_kernel(
         x_sc_win = sb.tile([P, T], U8, name="x_sc_win", align_bytes=64)
         nc.vector.memset(d_sc_win[:].bitcast(I32), 0)
         nc.gpsimd.memset(x_sc_win[:].bitcast(I32), 0)
-        nc.scalar.dma_start(d_sc_win[0:P:8, :].bitcast(I32), d_scales[0].bitcast(I32))
-        nc.scalar.dma_start(x_sc_win[0:P:8, :].bitcast(I32), x_scales[0].bitcast(I32))
 
         l_k1 = load_list(k1, "l_k1")
         l_offs = load_list(offs, "l_offs")
-        gs_raw = sb.tile([P, PACK], F32, name="gs_raw")
-        nc.sync.dma_start(gs_raw[:], gs.rearrange("(p t) o -> p (t o)", t=PACK))
         d_win = sb.tile([P, G], I32, name="d_win", align_bytes=64)
-        x_win = sb.tile([P, T], I32, name="x_win", align_bytes=64)
-        nc.sync.dma_start(d_win[:], d_words[0].rearrange("p n t -> p (n t)").bitcast(I32))
-        nc.sync.dma_start(x_win[:], x_words[0].rearrange("p n t -> p (n t)").bitcast(I32))
+        d_flat = d_words[0].rearrange("p n t -> p (n t)").bitcast(I32)
+        nc.sync.dma_start(d_win[:, 0:EARLY], d_flat[:, 0:EARLY])
         l_n2 = load_list(n2, "l_n2")
         l_n1 = load_list(n1, "l_n1")
+        nc.sync.dma_start(d_sc_win[0:P:8, :].bitcast(I32), d_scales[0].bitcast(I32))
+        nc.sync.dma_start(x_sc_win[0:P:8, :].bitcast(I32), x_scales[0].bitcast(I32))
+        x_win = sb.tile([P, T], I32, name="x_win", align_bytes=64)
+        nc.sync.dma_start(d_win[:, EARLY:G], d_flat[:, EARLY:G])
         l_n3 = load_list(n3, "l_n3")
+        nc.sync.dma_start(x_win[:], x_words[0].rearrange("p n t -> p (n t)").bitcast(I32))
         l_n4 = load_list(n4, "l_n4")
         l_n5 = load_list(n5, "l_n5")
         l_cand = load_list(cand, "l_cand")
-
-        gs16 = sb.tile([P, PACK], F32, name="gs16")
-        nc.scalar.activation(gs16[:], gs_raw[:], COPY, scale=0.0625)
 
         first_rows = sb.tile([P, H + S], U8, name="first_rows", align_bytes=64)
         cand_rows = sb.tile([P, C], U8, name="cand_rows", align_bytes=64)
         nc.gpsimd.memset(first_rows[:].bitcast(I32), 0)
         nc.gpsimd.memset(cand_rows[:].bitcast(I32), 0)
+        z_plane = sb.tile([P, S], U8, name="z_plane", align_bytes=64)
+        nc.gpsimd.memset(z_plane[:].bitcast(I32), 0)
 
-        def move_rows(queue, dst, src):
+        def move_rows(queues, dst, src):
             for r in range(4):
-                queue.dma_start(dst[r:P:32, :].bitcast(I32), src[8 * r : P : 32, :].bitcast(I32))
+                queues[r % len(queues)].dma_start(dst[r:P:32, :].bitcast(I32), src[8 * r : P : 32, :].bitcast(I32))
 
         def deal(dst, src, per_line, first, stop):
             nc.vector.tensor_copy(
@@ -80,17 +80,18 @@ def tile_picked_hpqhswapdsendhop_none_po_kernel(
         first_bytes = sb.tile([P, H + S], U8, name="first_bytes", align_bytes=64)
         nc.vector.tensor_copy(first_bytes[:, 0:H], d_sc_win[:].indirect(l_k1[:]))
         nc.vector.tensor_copy(first_bytes[:, H : H + S], x_sc_win[:].indirect(l_offs[:]))
-        move_rows(nc.scalar, first_rows, first_bytes)
+        move_rows([nc.sync, nc.scalar], first_rows, first_bytes)
 
-        d_picked = sb.tile([P, H], U32, name="d_picked", align_bytes=64)
+        d_picked = sb.tile([P, H], U32, name="d_picked", tag="d_picked", align_bytes=64)
         d_codes = sb.tile([P, H], U32, name="d_codes", align_bytes=64)
         d_plane = sb.tile([P, H], U8, name="d_plane", align_bytes=64)
         xq_codes = sb.tile([P, S], U32, name="xq_codes", align_bytes=64)
         nc.vector.tensor_copy(d_picked[:], d_win[:].bitcast(U32).indirect(l_k1[:]))
         nc.vector.tensor_copy(xq_codes[:], x_win[:].bitcast(U32).indirect(l_offs[:]))
-        deal(d_codes[:], d_picked[:], 4, 0, 1)
+        deal(d_codes[:], d_picked[:], 4, 0, PACK)
+        gs_raw = sb.tile([P, PACK], F32, name="gs_raw", tag="d_picked", align_bytes=64)
+        nc.sync.dma_start(gs_raw[:], gs.rearrange("(p t) o -> p (t o)", t=PACK))
         deal(d_plane[:], first_rows[:, 0:H], 16, 0, 1)
-        deal(d_codes[:], d_picked[:], 4, 1, PACK)
         deal(d_plane[:], first_rows[:, 0:H], 16, 1, PACK)
 
         h = []
@@ -107,9 +108,9 @@ def tile_picked_hpqhswapdsendhop_none_po_kernel(
             )
             ht = sb.tile([P, S], F32, name=f"h{t}", align_bytes=64)
             if t == 0:
-                nc.scalar.copy(ht[:], acc[:])
+                nc.scalar.activation(ht[:], acc[:], COPY, scale=0.0625)
             else:
-                nc.vector.tensor_copy(ht[:], acc[:])
+                nc.vector.tensor_scalar(ht[:], acc[:], 0.0625, None, ALU.mult)
             h.append(ht)
 
         c_codes = sb.tile([P, C], U32, name="c_codes", align_bytes=64)
@@ -120,48 +121,45 @@ def tile_picked_hpqhswapdsendhop_none_po_kernel(
             for a in range(0, C, P):
                 nc.vector.tensor_copy(c_bytes[:, a : a + P], x_sc_win[:].indirect(entries(l_cand, a, P)))
             deal(c_dealt[:], c_bytes[:], 16, 0, PACK)
-            move_rows(nc.sync, cand_rows, c_dealt)
+            move_rows([nc.sync], cand_rows, c_dealt)
 
         def cand_words():
-            c_picked = sb.tile([P, C], U32, name="c_picked", tag="pa1", align_bytes=64)
+            c_picked = sb.tile([P, C], U32, name="c_picked", tag="rb0", align_bytes=64)
             for a in range(0, C, P):
                 nc.vector.tensor_copy(c_picked[:, a : a + P], x_win[:].bitcast(U32).indirect(entries(l_cand, a, P)))
             deal(c_codes[:], c_picked[:], 4, 0, PACK)
 
-        pa = [sb.tile([P, W], F32, name=f"pa{t}", tag=f"pa{t}", align_bytes=64) for t in range(PACK)]
-        pb = [sb.tile([P, W], F32, name=f"pb{t}") for t in range(PACK)]
-        rb = [sb.tile([P, W], F32, name=f"rb{t}") for t in range(PACK)]
+        pa, pb = [], []
+        rb = [sb.tile([P, W], F32, name=f"rb{t}", tag=f"rb{t}", align_bytes=64) for t in range(PACK)]
         dt = []
         hop = [sb.tile([P, S], F32, name=f"hop{t}") for t in range(PACK)]
+        last = PACK - 1
         top = [sb.tile([P, S], F32, name=f"top{t}") for t in range(PACK)]
         z_bf = sb.tile([P, S, PACK], BF16, name="z_bf", align_bytes=64)
         z_codes = sb.tile([P, S], U32, name="z_codes", align_bytes=64)
-        z_plane = sb.tile([P, S], U8, name="z_plane", align_bytes=64)
-        nc.gpsimd.memset(z_plane[:].bitcast(I32), 0)
 
         def fetch_pairs(t):
+            pa.append(sb.tile([P, W], F32, name=f"pa{t}", tag=f"pa{min(t, 1)}", align_bytes=64))
+            pb.append(sb.tile([P, W], F32, name=f"pb{t}", tag=f"pb{min(t, 1)}", align_bytes=64))
             nc.scalar.activation(pb[t][:], h[t][:].indirect(l_n2[:]), COPY)
             nc.scalar.activation(pa[t][:], h[t][:].indirect(l_n1[:]), COPY)
             nc.vector.tensor_tensor(rb[t][:], pa[t][:], pb[t][:], ALU.subtract)
 
         def put_pb(t):
-            dt.append(sb.tile([P, S + 16], F32, name=f"dt{t}", tag="dt", bufs=2))
+            dt.append(sb.tile([P, S + 16], F32, name=f"dt{t}", align_bytes=64))
             nc.scalar.activation(dt[t][:].indirect(l_n1[:]), pb[t][:], COPY)
 
         def put_rb(t):
             nc.scalar.activation(dt[t][:].indirect(l_n2[:]), rb[t][:], COPY)
 
-        def hop_half(t, u):
-            cols = slice(u * HALF, (u + 1) * HALF)
-            nc.scalar.activation(hop[t][:, cols], dt[t][:].indirect(entries(l_n3, u * HALF, HALF)), COPY)
-
-        def top_part(t, first, count):
+        def hop_part(t, first, count, dst):
+            nc.scalar.activation(dst, dt[t][:].indirect(entries(l_n3, first, count)), COPY)
             cols = slice(first, first + count)
-            nc.vector.scalar_tensor_tensor(top[t][:, cols], hop[t][:, cols], 0.5, dt[t][:, cols], ALU.mult, ALU.max)
+            nc.vector.scalar_tensor_tensor(top[t][:, cols], dst, 0.5, dt[t][:, cols], ALU.mult, ALU.max)
 
         def z_part(t, first, count):
             cols = slice(first, first + count)
-            nc.vector.tensor_scalar(z_bf[:, cols, t], top[t][:, cols], gs16[:, t : t + 1], None, ALU.mult)
+            nc.vector.tensor_scalar(z_bf[:, cols, t], top[t][:, cols], gs_raw[:, t : t + 1], None, ALU.mult)
 
         def quantise_z(u):
             cols = slice(u * HALF, (u + 1) * HALF)
@@ -179,9 +177,9 @@ def tile_picked_hpqhswapdsendhop_none_po_kernel(
             put_rb(t)
             if t + 1 < PACK:
                 put_pb(t + 1)
-                nc.scalar.activation(hop[t][:], dt[t][:].indirect(l_n3[:]), COPY)
-                top_part(t, 0, S)
-                z_part(t, 0, S)
+                count = S if t + 1 < last else HALF
+                hop_part(t, 0, count, hop[t][:, 0:count])
+                z_part(t, 0, count)
             if t == 0:
                 cand_bytes()
             if t == 1:
@@ -203,10 +201,11 @@ def tile_picked_hpqhswapdsendhop_none_po_kernel(
             )
             return acc
 
-        last = PACK - 1
-        for u in range(2):
-            hop_half(last, u)
-            top_part(last, u * HALF, HALF)
+        late_hop = sb.tile([P, HALF], F32, name="late_hop", tag="pa1", align_bytes=64)
+        hop_part(last - 1, HALF, HALF, late_hop[:])
+        hop_part(last, 0, HALF, hop[last][:, 0:HALF])
+        z_part(last - 1, HALF, HALF)
+        hop_part(last, HALF, HALF, hop[last][:, HALF:S])
         for u in range(2):
             z_part(last, u * HALF, HALF)
         for u in range(2):
@@ -239,6 +238,7 @@ def tile_picked_hpqhswapdsendhop_none_po_kernel(
             for cols in parts:
                 nc.vector.tensor_copy(y_bf[:, cols, t], y[t][:, cols])
 
+        out_words = out_1[0].rearrange("p n t -> p (n t)").bitcast(I32)
         fetch_far(0)
         for t in range(PACK):
             if t + 1 < PACK:
@@ -252,7 +252,7 @@ def tile_picked_hpqhswapdsendhop_none_po_kernel(
                 scales=y_plane[:, cols],
                 in_=y_bf[:, cols, :].rearrange("p j t -> p (j t)"),
             )
-        nc.sync.dma_start(out_1[0].rearrange("p n t -> p (n t)").bitcast(I32), y_codes[:].bitcast(I32))
+            nc.sync.dma_start(out_words[:, cols], y_codes[:, cols].bitcast(I32))
         for q in range(4):
-            queue = nc.scalar if q < 3 else nc.sync
+            queue = nc.scalar if q < 2 else nc.sync
             queue.dma_start(out_2[0, 4 * q : 4 * q + 4, :].bitcast(I32), y_plane[32 * q : 32 * q + 4, :].bitcast(I32))

@@ -18,7 +18,7 @@ COPY = mybir.ActivationFunctionType.Copy
 P = 128
 PACK = 4
 HALF = S // 2
-EARLY = G // 4
+EARLY = G // 8
 
 
 def tile_picked_hpqhswapdsendhop_none_po_kernel(
@@ -95,22 +95,27 @@ def tile_picked_hpqhswapdsendhop_none_po_kernel(
         deal(d_plane[:], first_rows[:, 0:H], 16, 1, PACK)
 
         h = []
-        for t in range(PACK):
-            acc = ps.tile([P, S], F32, name=f"h_acc{t}", tag=f"bank{t}")
+
+        def layer(t, first, count, bank):
+            acc = ps.tile([P, count], F32, name=f"h_acc{t}_{first}", tag=f"bank{bank}")
             nc.tensor.matmul_mx(
                 out=acc[:],
                 lhsT=d_codes[:, t * P : (t + 1) * P].bitcast(FP8X4),
                 lhsT_scale=d_plane[:, t * P : (t + 1) * P],
-                rhs=xq_codes[:].bitcast(FP8X4),
-                rhs_scale=first_rows[:, H : H + S],
+                rhs=xq_codes[:, first : first + count].bitcast(FP8X4),
+                rhs_scale=first_rows[:, H + first : H + first + count],
                 start=True,
                 stop=True,
             )
+            return acc
+
+        for t in range(PACK):
             ht = sb.tile([P, S], F32, name=f"h{t}", align_bytes=64)
             if t == 0:
-                nc.scalar.activation(ht[:], acc[:], COPY, scale=0.0625)
+                nc.vector.tensor_scalar(ht[:, 0:HALF], layer(t, 0, HALF, 0)[:], 0.0625, None, ALU.mult)
+                nc.scalar.activation(ht[:, HALF:S], layer(t, HALF, HALF, 4)[:], COPY, scale=0.0625)
             else:
-                nc.vector.tensor_scalar(ht[:], acc[:], 0.0625, None, ALU.mult)
+                nc.vector.tensor_scalar(ht[:], layer(t, 0, S, t)[:], 0.0625, None, ALU.mult)
             h.append(ht)
 
         c_codes = sb.tile([P, C], U32, name="c_codes", align_bytes=64)
@@ -235,8 +240,11 @@ def tile_picked_hpqhswapdsendhop_none_po_kernel(
             for cols in parts:
                 nc.vector.tensor_tensor(y[t][:, cols], sent[t][:, cols], s[t][:, cols], ALU.subtract)
             nc.sync.dma_start(out_rows[:, t, :], y[t][:])
-            for cols in parts:
-                nc.vector.tensor_copy(y_bf[:, cols, t], y[t][:, cols])
+            if t < last:
+                nc.vector.tensor_tensor(y_bf[:, :, t], sent[t][:, 0:S], s[t][:, 0:S], ALU.subtract)
+            else:
+                for cols in parts:
+                    nc.vector.tensor_copy(y_bf[:, cols, t], y[t][:, cols])
 
         out_words = out_1[0].rearrange("p n t -> p (n t)").bitcast(I32)
         fetch_far(0)

@@ -18,7 +18,7 @@ COPY = mybir.ActivationFunctionType.Copy
 P = 128
 PACK = 4
 HALF = S // 2
-EARLY = G // 8
+EARLY = 3 * G // 16
 
 
 def tile_picked_hpqhswapdsendhop_none_po_kernel(
@@ -41,7 +41,7 @@ def tile_picked_hpqhswapdsendhop_none_po_kernel(
         d_sc_win = sb.tile([P, G], U8, name="d_sc_win", align_bytes=64)
         x_sc_win = sb.tile([P, T], U8, name="x_sc_win", align_bytes=64)
         nc.vector.memset(d_sc_win[:].bitcast(I32), 0)
-        nc.gpsimd.memset(x_sc_win[:].bitcast(I32), 0)
+        nc.vector.memset(x_sc_win[:].bitcast(I32), 0)
 
         l_k1 = load_list(k1, "l_k1")
         l_offs = load_list(offs, "l_offs")
@@ -62,10 +62,10 @@ def tile_picked_hpqhswapdsendhop_none_po_kernel(
 
         first_rows = sb.tile([P, H + S], U8, name="first_rows", align_bytes=64)
         cand_rows = sb.tile([P, C], U8, name="cand_rows", align_bytes=64)
-        nc.gpsimd.memset(first_rows[:].bitcast(I32), 0)
-        nc.gpsimd.memset(cand_rows[:].bitcast(I32), 0)
+        nc.vector.memset(first_rows[:].bitcast(I32), 0)
+        nc.vector.memset(cand_rows[:].bitcast(I32), 0)
         z_plane = sb.tile([P, S], U8, name="z_plane", align_bytes=64)
-        nc.gpsimd.memset(z_plane[:].bitcast(I32), 0)
+        nc.vector.memset(z_plane[:].bitcast(I32), 0)
 
         def move_rows(queues, dst, src):
             for r in range(4):
@@ -73,26 +73,29 @@ def tile_picked_hpqhswapdsendhop_none_po_kernel(
 
         def deal(dst, src, per_line, first, stop):
             nc.vector.tensor_copy(
-                dst.rearrange("p (t a i) -> p a t i", t=PACK, i=per_line)[:, :, first:stop, :],
+                dst.rearrange("p (t a i) -> p a t i", t=stop - first, i=per_line),
                 src.rearrange("p (a i t) -> p a t i", t=PACK, i=per_line)[:, :, first:stop, :],
             )
 
-        first_bytes = sb.tile([P, H + S], U8, name="first_bytes", align_bytes=64)
+        first_bytes = sb.tile([P, H + S], U8, name="first_bytes", tag="first_bytes", align_bytes=64)
         nc.vector.tensor_copy(first_bytes[:, 0:H], d_sc_win[:].indirect(l_k1[:]))
         nc.vector.tensor_copy(first_bytes[:, H : H + S], x_sc_win[:].indirect(l_offs[:]))
         move_rows([nc.sync, nc.scalar], first_rows, first_bytes)
 
         d_picked = sb.tile([P, H], U32, name="d_picked", tag="d_picked", align_bytes=64)
-        d_codes = sb.tile([P, H], U32, name="d_codes", align_bytes=64)
+        d_codes0 = sb.tile([P, P], U32, name="d_codes0", align_bytes=64)
+        d_codes_rest = sb.tile([P, H - P], U32, name="d_codes_rest", tag="first_bytes", align_bytes=64)
+        d_codes = [d_codes0[:]] + [d_codes_rest[:, a : a + P] for a in range(0, H - P, P)]
         d_plane = sb.tile([P, H], U8, name="d_plane", align_bytes=64)
         xq_codes = sb.tile([P, S], U32, name="xq_codes", align_bytes=64)
         nc.vector.tensor_copy(d_picked[:], d_win[:].bitcast(U32).indirect(l_k1[:]))
         nc.vector.tensor_copy(xq_codes[:], x_win[:].bitcast(U32).indirect(l_offs[:]))
-        deal(d_codes[:], d_picked[:], 4, 0, PACK)
+        deal(d_codes0[:], d_picked[:], 4, 0, 1)
+        deal(d_plane[:, 0:P], first_rows[:, 0:H], 16, 0, 1)
+        deal(d_codes_rest[:], d_picked[:], 4, 1, PACK)
+        deal(d_plane[:, P:H], first_rows[:, 0:H], 16, 1, PACK)
         gs_raw = sb.tile([P, PACK], F32, name="gs_raw", tag="d_picked", align_bytes=64)
         nc.sync.dma_start(gs_raw[:], gs.rearrange("(p t) o -> p (t o)", t=PACK))
-        deal(d_plane[:], first_rows[:, 0:H], 16, 0, 1)
-        deal(d_plane[:], first_rows[:, 0:H], 16, 1, PACK)
 
         h = []
 
@@ -100,7 +103,7 @@ def tile_picked_hpqhswapdsendhop_none_po_kernel(
             acc = ps.tile([P, count], F32, name=f"h_acc{t}_{first}", tag=f"bank{bank}")
             nc.tensor.matmul_mx(
                 out=acc[:],
-                lhsT=d_codes[:, t * P : (t + 1) * P].bitcast(FP8X4),
+                lhsT=d_codes[t].bitcast(FP8X4),
                 lhsT_scale=d_plane[:, t * P : (t + 1) * P],
                 rhs=xq_codes[:, first : first + count].bitcast(FP8X4),
                 rhs_scale=first_rows[:, H + first : H + first + count],
@@ -112,8 +115,7 @@ def tile_picked_hpqhswapdsendhop_none_po_kernel(
         for t in range(PACK):
             ht = sb.tile([P, S], F32, name=f"h{t}", align_bytes=64)
             if t == 0:
-                nc.vector.tensor_scalar(ht[:, 0:HALF], layer(t, 0, HALF, 0)[:], 0.0625, None, ALU.mult)
-                nc.scalar.activation(ht[:, HALF:S], layer(t, HALF, HALF, 4)[:], COPY, scale=0.0625)
+                nc.scalar.activation(ht[:], layer(t, 0, S, t)[:], COPY, scale=0.0625)
             else:
                 nc.vector.tensor_scalar(ht[:], layer(t, 0, S, t)[:], 0.0625, None, ALU.mult)
             h.append(ht)

from contextlib import ExitStack

import concourse.mybir as mybir

K, T, S, G, H, W, C = 512, 1024, 256, 2048, 512, 128, 512
FLOPS = 2 * K * H * S + 2 * K * C * S

F32 = mybir.dt.float32
BF16 = mybir.dt.bfloat16
I32 = mybir.dt.int32
U32 = mybir.dt.uint32
U16 = mybir.dt.uint16
U8 = mybir.dt.uint8
FP8X4 = mybir.dt.float8_e4m3fn_x4
ALU = mybir.AluOpType
COPY = mybir.ActivationFunctionType.Copy

P = 128
PACK = 4
HALF = S // 2
EARLY = 3 * G // 16


def tile_picked_hpqhswapdsendhop_none_po_kernel(
    tc, x_words, x_scales, d_words, d_scales, gs, offs, k1, n1, n2, n3, cand, n4, n5, out_0, out_1, out_2
):
    nc = tc.nc
    with ExitStack() as ctx:
        lists = ctx.enter_context(tc.tile_pool(name="lists", bufs=1))
        sb = ctx.enter_context(tc.tile_pool(name="sb", bufs=1))
        ps = ctx.enter_context(tc.psum_pool(name="ps", bufs=1))

        def load_list(src, name):
            t = lists.tile(list(src.shape), U16, name=name)
            nc.sync.dma_start(t[:], src)
            return t

        def entries(lst, first, count):
            return lst[:, first // 16 : (first + count) // 16]

        d_sc_win = sb.tile([P, G], U8, name="d_sc_win", align_bytes=64)
        x_sc_win = sb.tile([P, T], U8, name="x_sc_win", align_bytes=64)
        nc.vector.memset(d_sc_win[:].bitcast(I32), 0)
        nc.vector.memset(x_sc_win[:].bitcast(I32), 0)

        l_k1 = load_list(k1, "l_k1")
        l_offs = load_list(offs, "l_offs")
        d_win = sb.tile([P, G], I32, name="d_win", align_bytes=64)
        d_flat = d_words[0].rearrange("p n t -> p (n t)").bitcast(I32)
        nc.sync.dma_start(d_win[:, 0:EARLY], d_flat[:, 0:EARLY])
        l_n2 = load_list(n2, "l_n2")
        l_n1 = load_list(n1, "l_n1")
        nc.sync.dma_start(d_sc_win[0:P:8, :].bitcast(I32), d_scales[0].bitcast(I32))
        nc.sync.dma_start(x_sc_win[0:P:8, :].bitcast(I32), x_scales[0].bitcast(I32))
        x_win = sb.tile([P, T], I32, name="x_win", align_bytes=64)
        nc.sync.dma_start(d_win[:, EARLY:G], d_flat[:, EARLY:G])
        l_n3 = load_list(n3, "l_n3")
        nc.sync.dma_start(x_win[:], x_words[0].rearrange("p n t -> p (n t)").bitcast(I32))
        l_n4 = load_list(n4, "l_n4")
        l_n5 = load_list(n5, "l_n5")
        l_cand = load_list(cand, "l_cand")

        first_rows = sb.tile([P, H + S], U8, name="first_rows", align_bytes=64)
        cand_rows = sb.tile([P, C], U8, name="cand_rows", align_bytes=64)
        nc.vector.memset(first_rows[:].bitcast(I32), 0)
        nc.vector.memset(cand_rows[:].bitcast(I32), 0)
        z_plane = sb.tile([P, S], U8, name="z_plane", align_bytes=64)
        nc.vector.memset(z_plane[:].bitcast(I32), 0)

        def move_rows(queues, dst, src):
            for r in range(4):
                queues[r % len(queues)].dma_start(dst[r:P:32, :].bitcast(I32), src[8 * r : P : 32, :].bitcast(I32))

        def deal(dst, src, per_line, first, stop):
            nc.vector.tensor_copy(
                dst.rearrange("p (t a i) -> p a t i", t=stop - first, i=per_line),
                src.rearrange("p (a i t) -> p a t i", t=PACK, i=per_line)[:, :, first:stop, :],
            )

        first_bytes = sb.tile([P, H + S], U8, name="first_bytes", tag="first_bytes", align_bytes=64)
        nc.vector.tensor_copy(first_bytes[:, 0:H], d_sc_win[:].indirect(l_k1[:]))
        nc.vector.tensor_copy(first_bytes[:, H : H + S], x_sc_win[:].indirect(l_offs[:]))
        move_rows([nc.sync, nc.scalar], first_rows, first_bytes)

        d_picked = sb.tile([P, H], U32, name="d_picked", tag="d_picked", align_bytes=64)
        d_codes0 = sb.tile([P, P], U32, name="d_codes0", align_bytes=64)
        d_codes_rest = sb.tile([P, H - P], U32, name="d_codes_rest", tag="first_bytes", align_bytes=64)
        d_codes = [d_codes0[:]] + [d_codes_rest[:, a : a + P] for a in range(0, H - P, P)]
        d_plane = sb.tile([P, H], U8, name="d_plane", align_bytes=64)
        xq_codes = sb.tile([P, S], U32, name="xq_codes", align_bytes=64)
        nc.vector.tensor_copy(d_picked[:], d_win[:].bitcast(U32).indirect(l_k1[:]))
        nc.vector.tensor_copy(xq_codes[:], x_win[:].bitcast(U32).indirect(l_offs[:]))
        deal(d_codes0[:], d_picked[:], 4, 0, 1)
        deal(d_plane[:, 0:P], first_rows[:, 0:H], 16, 0, 1)
        deal(d_codes_rest[:], d_picked[:], 4, 1, PACK)
        deal(d_plane[:, P:H], first_rows[:, 0:H], 16, 1, PACK)
        gs_raw = sb.tile([P, PACK], F32, name="gs_raw", tag="d_picked", align_bytes=64)
        nc.sync.dma_start(gs_raw[:], gs.rearrange("(p t) o -> p (t o)", t=PACK))

        h = []

        def layer(t, first, count, bank):
            acc = ps.tile([P, count], F32, name=f"h_acc{t}_{first}", tag=f"bank{bank}")
            nc.tensor.matmul_mx(
                out=acc[:],
                lhsT=d_codes[t].bitcast(FP8X4),
                lhsT_scale=d_plane[:, t * P : (t + 1) * P],
                rhs=xq_codes[:, first : first + count].bitcast(FP8X4),
                rhs_scale=first_rows[:, H + first : H + first + count],
                start=True,
                stop=True,
            )
            return acc

        for t in range(PACK):
            ht = sb.tile([P, S], F32, name=f"h{t}", align_bytes=64)
            if t == 0:
                nc.scalar.activation(ht[:], layer(t, 0, S, t)[:], COPY, scale=0.0625)
            else:
                nc.vector.tensor_scalar(ht[:], layer(t, 0, S, t)[:], 0.0625, None, ALU.mult)
            h.append(ht)

        c_codes = sb.tile([P, C], U32, name="c_codes", align_bytes=64)
        c_dealt = sb.tile([P, C], U8, name="c_dealt", align_bytes=64)

        def cand_bytes():
            c_bytes = sb.tile([P, C], U8, name="c_bytes", tag="pa0", align_bytes=64)
            for a in range(0, C, P):
                nc.vector.tensor_copy(c_bytes[:, a : a + P], x_sc_win[:].indirect(entries(l_cand, a, P)))
            deal(c_dealt[:], c_bytes[:], 16, 0, PACK)
            move_rows([nc.sync], cand_rows, c_dealt)

        def cand_words():
            c_picked = sb.tile([P, C], U32, name="c_picked", tag="rb0", align_bytes=64)
            for a in range(0, C, P):
                nc.vector.tensor_copy(c_picked[:, a : a + P], x_win[:].bitcast(U32).indirect(entries(l_cand, a, P)))
            deal(c_codes[:], c_picked[:], 4, 0, PACK)

        pa, pb = [], []
        rb = [sb.tile([P, W], F32, name=f"rb{t}", tag=f"rb{t}", align_bytes=64) for t in range(PACK)]
        dt = []
        hop = [sb.tile([P, S], F32, name=f"hop{t}") for t in range(PACK)]
        last = PACK - 1
        top = [sb.tile([P, S], F32, name=f"top{t}") for t in range(PACK)]
        z_bf = sb.tile([P, S, PACK], BF16, name="z_bf", align_bytes=64)
        z_codes = sb.tile([P, S], U32, name="z_codes", align_bytes=64)

        def fetch_pairs(t):
            pa.append(sb.tile([P, W], F32, name=f"pa{t}", tag=f"pa{min(t, 1)}", align_bytes=64))
            pb.append(sb.tile([P, W], F32, name=f"pb{t}", tag=f"pb{min(t, 1)}", align_bytes=64))
            nc.scalar.activation(pb[t][:], h[t][:].indirect(l_n2[:]), COPY)
            nc.scalar.activation(pa[t][:], h[t][:].indirect(l_n1[:]), COPY)
            nc.vector.tensor_tensor(rb[t][:], pa[t][:], pb[t][:], ALU.subtract)

        def put_pb(t):
            dt.append(sb.tile([P, S + 16], F32, name=f"dt{t}", align_bytes=64))
            nc.scalar.activation(dt[t][:].indirect(l_n1[:]), pb[t][:], COPY)

        def put_rb(t):
            nc.scalar.activation(dt[t][:].indirect(l_n2[:]), rb[t][:], COPY)

        def hop_part(t, first, count, dst):
            nc.scalar.activation(dst, dt[t][:].indirect(entries(l_n3, first, count)), COPY)
            cols = slice(first, first + count)
            nc.vector.scalar_tensor_tensor(top[t][:, cols], dst, 0.5, dt[t][:, cols], ALU.mult, ALU.max)

        def z_part(t, first, count):
            cols = slice(first, first + count)
            nc.vector.tensor_scalar(z_bf[:, cols, t], top[t][:, cols], gs_raw[:, t : t + 1], None, ALU.mult)

        def quantise_z(u):
            cols = slice(u * HALF, (u + 1) * HALF)
            nc.vector.quantize_mx(
                out=z_codes[:, cols].bitcast(FP8X4),
                scales=z_plane[:, cols],
                in_=z_bf[:, cols, :].rearrange("p j t -> p (j t)"),
            )

        fetch_pairs(0)
        put_pb(0)
        for t in range(PACK):
            if t + 1 < PACK:
                fetch_pairs(t + 1)
            put_rb(t)
            if t + 1 < PACK:
                put_pb(t + 1)
                count = S if t + 1 < last else HALF
                hop_part(t, 0, count, hop[t][:, 0:count])
                z_part(t, 0, count)
            if t == 0:
                cand_bytes()
            if t == 1:
                cand_words()

        s = [sb.tile([P, S + 16], F32, name=f"s{t}", align_bytes=64) for t in range(PACK)]

        def score(t, first, count, bank):
            cols = slice(first, first + count)
            acc = ps.tile([P, count], F32, name=f"s_acc{t}_{first}", tag=f"bank{bank}")
            nc.tensor.matmul_mx(
                out=acc[:],
                lhsT=c_codes[:, t * P : (t + 1) * P].bitcast(FP8X4),
                lhsT_scale=cand_rows[:, t * P : (t + 1) * P],
                rhs=z_codes[:, cols].bitcast(FP8X4),
                rhs_scale=z_plane[:, cols],
                start=True,
                stop=True,
            )
            return acc

        late_hop = sb.tile([P, HALF], F32, name="late_hop", tag="pa1", align_bytes=64)
        hop_part(last - 1, HALF, HALF, late_hop[:])
        hop_part(last, 0, HALF, hop[last][:, 0:HALF])
        z_part(last - 1, HALF, HALF)
        hop_part(last, HALF, HALF, hop[last][:, HALF:S])
        for u in range(2):
            z_part(last, u * HALF, HALF)
        for u in range(2):
            quantise_z(u)
            acc = score(0, u * HALF, HALF, 4 + u)
            nc.scalar.activation(s[0][:, u * HALF : (u + 1) * HALF], acc[:], COPY, scale=0.0625)
        for t in range(1, PACK):
            acc = score(t, 0, S, (5 + t) % 8)
            nc.vector.tensor_scalar(s[t][:, 0:S], acc[:], 0.0625, None, ALU.mult)

        far = [sb.tile([P, S], F32, name=f"far{t}") for t in range(PACK)]
        st = [sb.tile([P, S], F32, name=f"st{t}") for t in range(PACK)]
        sent = [sb.tile([P, S + 96], F32, name=f"sent{t}") for t in range(PACK)]
        y = [sb.tile([P, S], F32, name=f"y{t}") for t in range(PACK)]
        y_bf = sb.tile([P, S, PACK], BF16, name="y_bf", align_bytes=64)
        y_codes = sb.tile([P, S], U32, name="y_codes", align_bytes=64)
        y_plane = sb.tile([P, S], U8, name="y_plane", align_bytes=64)
        out_rows = out_0.rearrange("(p t) j -> p t j", t=PACK)

        def fetch_far(t):
            nc.scalar.activation(far[t][:], s[t][:].indirect(l_n4[:]), COPY)
            nc.vector.tensor_tensor(st[t][:], far[t][:], s[t][:, 0:S], ALU.max)

        def send(t):
            nc.scalar.activation(sent[t][:].indirect(l_n5[:]), st[t][:], COPY)
            parts = [slice(0, S)] if t < last else [slice(0, HALF), slice(HALF, S)]
            for cols in parts:
                nc.vector.tensor_tensor(y[t][:, cols], sent[t][:, cols], s[t][:, cols], ALU.subtract)
            nc.sync.dma_start(out_rows[:, t, :], y[t][:])
            if t < last:
                nc.vector.tensor_tensor(y_bf[:, :, t], sent[t][:, 0:S], s[t][:, 0:S], ALU.subtract)
            else:
                for cols in parts:
                    nc.vector.tensor_copy(y_bf[:, cols, t], y[t][:, cols])

        out_words = out_1[0].rearrange("p n t -> p (n t)").bitcast(I32)
        fetch_far(0)
        for t in range(PACK):
            if t + 1 < PACK:
                fetch_far(t + 1)
            send(t)

        for u in range(2):
            cols = slice(u * HALF, (u + 1) * HALF)
            nc.vector.quantize_mx(
                out=y_codes[:, cols].bitcast(FP8X4),
                scales=y_plane[:, cols],
                in_=y_bf[:, cols, :].rearrange("p j t -> p (j t)"),
            )
            nc.sync.dma_start(out_words[:, cols], y_codes[:, cols].bitcast(I32))
        for q in range(4):
            queue = nc.scalar if q < 2 else nc.sync
            queue.dma_start(out_2[0, 4 * q : 4 * q + 4, :].bitcast(I32), y_plane[32 * q : 32 * q + 4, :].bitcast(I32))
